import numpy as np
import ml_dtypes


def mxq(x, axis, fmt="e4m3"):
    dtype, down = {"e4m3": (ml_dtypes.float8_e4m3fn, 7), "e5m2": (ml_dtypes.float8_e5m2, 14)}[fmt]
    v = np.moveaxis(np.asarray(x, np.float32).astype(ml_dtypes.bfloat16).astype(np.float64), axis, -1)
    blocks = v.reshape(v.shape[:-1] + (-1, 32))
    amax = np.abs(blocks).max(-1, keepdims=True)
    byte = np.maximum(np.where(amax > 0, np.frexp(amax)[1] - 1 + 127, 0) - down, 1)
    scale = np.exp2(byte - 127.0)
    codes = (blocks / scale).astype(np.float32).astype(dtype).astype(np.float64)
    return np.moveaxis((codes * scale).reshape(v.shape), -1, axis)


WIDE = False


def mx_kscale(k):
    if not WIDE:
        return np.ones(k)
    levels = np.array([10, -10, 5, -5, 0])
    if k % 512:
        return np.exp2(np.random.permutation(np.resize(levels, k // 32))).repeat(32)
    a = np.empty((k // 512, 16))
    for p in range(k // 512):
        a[p, :8] = np.random.permutation(np.resize(levels, 8))
        for g in range(8):
            far = levels[np.abs(levels - a[p, g]) >= 10]
            a[p, g + 8] = far[np.random.randint(len(far))]
    return np.exp2(a.ravel()).repeat(32)


BF16 = ml_dtypes.bfloat16


def bf(x):
    return np.asarray(x, np.float32).astype(BF16)


def f64(x):
    return np.asarray(x).astype(np.float64)


E2M1 = np.array([0.0, 0.5, 1.0, 1.5, 2.0, 3.0, 4.0, 6.0, -0.0, -0.5, -1.0, -1.5, -2.0, -3.0, -4.0, -6.0])


def pack_weight(w, fmt):
    k, n = w.shape
    w = f64(bf(w)).reshape(k // 32, 32, n)
    amax = np.abs(w).max(1)
    if fmt == "e4m3":
        byte = np.frexp(amax)[1] - 1 + 127 - 7
    else:
        mant, ex = np.frexp(amax / 6.0)
        byte = np.where(mant > 0.5, ex, ex - 1) + 127
    byte = np.clip(np.where(amax > 0, byte, 1), 1, 254)
    scaled = (w * np.exp2(127.0 - byte)[:, None, :]).reshape(k, n).astype(np.float32)
    by_word = np.ascontiguousarray(scaled.reshape(k // 512, 128, 4, n).transpose(0, 1, 3, 2))
    if fmt == "e4m3":
        words = by_word.astype(ml_dtypes.float8_e4m3fn).view(np.uint8)
    else:
        c = by_word.astype(ml_dtypes.float4_e2m1fn).view(np.uint8) & 0xF
        words = c[..., 0::2] | (c[..., 1::2] << 4)
    return np.ascontiguousarray(words), np.ascontiguousarray(byte.astype(np.uint8).reshape(k // 512, 16, n))


def unpack_weight(words, scales, fmt):
    g, p, n, _ = words.shape
    if fmt == "e4m3":
        vals = np.ascontiguousarray(words).view(ml_dtypes.float8_e4m3fn).astype(np.float64)
    else:
        nib = np.empty((g, p, n, 4), np.uint8)
        nib[..., 0::2] = words & 0xF
        nib[..., 1::2] = words >> 4
        vals = E2M1[nib]
    vals = vals * np.repeat(np.exp2(scales.astype(np.float64) - 127.0), 8, axis=1)[..., None]
    return vals.transpose(0, 1, 3, 2).reshape(g * 512, n)
def pack4(w):
    words, scales = pack_weight(w, "e2m1")
    return words.reshape(words.shape[0], 128, -1), scales


def unpack4(words, scales):
    return unpack_weight(words.reshape(words.shape[0], 128, -1, 2), scales, "e2m1")


S, F, D, T = 1024, 1024, 512, 2048
MEAN_SHARP, DEV_SHARP = 2.0, 1.8


def setup_inputs():
    r, u = mx_kscale(F), mx_kscale(S)
    style = bf(np.random.standard_normal((S, F)) * r * u[:, None])
    w_value = bf(np.random.standard_normal((F, D)) / np.sqrt(F) / r[:, None])
    a = np.exp(MEAN_SHARP * np.random.standard_normal((S, T)))
    b = np.exp(DEV_SHARP * np.random.standard_normal((S, T)))
    mean_words, mean_scales = pack4(a / a.sum(axis=0) / u[:, None])
    dev_words, dev_scales = pack4(b / b.sum(axis=0) / (u * u)[:, None])
    content = bf(np.random.standard_normal((T, D)))
    return {"style": style, "w_value": w_value,
            "mean_words": mean_words, "mean_scales": mean_scales,
            "dev_words": dev_words, "dev_scales": dev_scales,
            "content": content}


def reference(style, w_value, mean_words, mean_scales, dev_words, dev_scales, content):
    v = mxq(f64(style), 1, "e4m3") @ mxq(f64(w_value), 0, "e4m3")
    a = unpack4(mean_words, mean_scales)
    mean = a.T @ mxq(v, 0, "e4m3")
    b = unpack4(dev_words, dev_scales)
    power = b.T @ mxq(np.square(v), 0, "e4m3")
    scaled = np.sqrt(power) * f64(content)
    return mean, scaled

@@ -1,0 +1,261 @@
+from contextlib import ExitStack
+
+import concourse.mybir as mybir
+from concourse.masks import make_identity
+
+S, F, D, T = 1024, 1024, 512, 2048
+FLOPS = 2 * S * F * D + 2 * 2 * T * S * D
+
+F32 = mybir.dt.float32
+BF16 = mybir.dt.bfloat16
+I32 = mybir.dt.int32
+U32 = mybir.dt.uint32
+U8 = mybir.dt.uint8
+FP8X4 = mybir.dt.float8_e4m3fn_x4
+FP4X4 = mybir.dt.float4_e2m1fn_x4
+ACT = mybir.ActivationFunctionType
+
+P = 128
+PACK = 4
+K_PASS = P * PACK
+PASSES = 2
+QUARTERS = D // P
+TILES = T // P
+STORES = ((1, 1, 2, 2, 2, 2, 2, 2, 1, 1), (2, 2, 2, 2, 2, 2, 2, 1, 1))
+CONTENT_TILES = 4
+MEAN_LEAD = 6
+
+
+def tile_adaattn_style_moments_s13_kernel(
+    tc, style, w_value, mean_words, mean_scales, dev_words, dev_scales, content, out_0, out_1
+):
+    nc = tc.nc
+    with ExitStack() as ctx:
+        keep = ctx.enter_context(tc.tile_pool(name="keep", bufs=1))
+        psum = ctx.enter_context(tc.psum_pool(name="psum", bufs=1))
+        ctx.enter_context(tc.manual_schedule())
+
+        def sb(name, shape, dtype):
+            return keep.tile(shape, dtype, name=name, align_bytes=64)
+
+        def bank(b):
+            return psum.tile([P, D], F32, name="bank%d" % b)
+
+        ident = sb("ident", [P, P], F32)
+        make_identity(nc, ident[:])
+        one = sb("one", [P, 8], F32)
+        root = sb("root", [P, 8], F32)
+        nc.gpsimd.memset(one[:], 1.0)
+        nc.scalar.activation(out=root[:], in_=one[:], func=ACT.Sqrt)
+
+        planes = [sb("plane%d" % a, [P, PASSES, T], U8) for a in range(2)]
+        for a in range(2):
+            nc.vector.memset(planes[a][:].rearrange("p g n -> p (g n)").bitcast(I32), 0)
+
+        w_raw = [sb("w_raw%d" % c, [P, PACK, D], BF16) for c in range(PASSES)]
+        s_raw = [sb("s_raw%d" % h, [P, 2, F], BF16) for h in range(4)]
+
+        def load_w(c):
+            nc.sync.dma_start(
+                out=w_raw[c][:], in_=w_value[c * K_PASS : (c + 1) * K_PASS, :].rearrange("(p j) d -> p j d", j=PACK)
+            )
+
+        def load_s(h):
+            g, half = divmod(h, 2)
+            rows = style[g * K_PASS : (g + 1) * K_PASS, :].rearrange("(m t) k -> m t k", t=PACK)
+            nc.sync.dma_start(out=s_raw[h][:], in_=rows[:, 2 * half : 2 * half + 2, :])
+
+        load_w(0)
+        load_s(0)
+        load_w(1)
+        load_s(1)
+        load_s(2)
+        load_s(3)
+
+        words = [sb("words%d" % a, [P, PASSES, 2 * T], U8) for a in range(2)]
+        for a, (w_hbm, s_hbm) in enumerate(((mean_words, mean_scales), (dev_words, dev_scales))):
+            nc.sync.dma_start(out=words[a][:].bitcast(I32), in_=w_hbm.rearrange("g p n -> p g n").bitcast(I32))
+        for a, (w_hbm, s_hbm) in enumerate(((mean_words, mean_scales), (dev_words, dev_scales))):
+            rows = s_hbm.rearrange("g q n -> q g n").bitcast(I32)
+            for quad in range(4):
+                nc.sync.dma_start(
+                    out=planes[a][32 * quad : 32 * quad + 4, :, :].bitcast(I32), in_=rows[4 * quad : 4 * quad + 4, :, :]
+                )
+        cont = [sb("cont%d" % i, [P, CONTENT_TILES, D], BF16) for i in range(TILES // CONTENT_TILES)]
+        for i in range(TILES // CONTENT_TILES):
+            rows = content[i * CONTENT_TILES * P : (i + 1) * CONTENT_TILES * P, :]
+            nc.sync.dma_start(out=cont[i][:], in_=rows.rearrange("(a p) d -> p a d", p=P))
+
+        w_grp = [sb("w_grp%d" % c, [P, D, PACK], BF16) for c in range(PASSES)]
+        w_codes = [sb("w_codes%d" % c, [P, D], U32) for c in range(PASSES)]
+        w_scales = [sb("w_scales%d" % c, [P, D], U8) for c in range(PASSES)]
+        s_grp = [sb("s_grp%d" % h, [P, 2, PASSES, P, 2], F32) for h in range(4)]
+        s_codes = [sb("s_codes%d" % h, [P, 2 * PASSES * P], U32) for h in range(4)]
+        s_scales = [sb("s_scales%d" % h, [P, 2 * PASSES * P], U8) for h in range(4)]
+        v_grp = [[[sb("v_grp%d%d%d" % (a, g, x), [P, D // 2, PACK], BF16) for x in range(2)] for g in range(PASSES)] for a in range(2)]
+        v_codes = [[sb("v_codes%d%d" % (a, g), [P, D], U32) for g in range(PASSES)] for a in range(2)]
+        v_scales = [[sb("v_scales%d%d" % (a, g), [P, D], U8) for g in range(PASSES)] for a in range(2)]
+
+        def interleave_w(c):
+            nc.vector.tensor_copy(
+                out=w_grp[c][:].rearrange("p (c i) j -> p c j i", i=4),
+                in_=w_raw[c][:].rearrange("p j (c i) -> p c j i", i=4),
+            )
+
+        def quant_w(c):
+            nc.vector.quantize_mx(
+                out=w_codes[c][:].bitcast(FP8X4), scales=w_scales[c][:], in_=w_grp[c][:].rearrange("p d j -> p (d j)")
+            )
+
+        def turn_s(h):
+            for e in range(2):
+                xt = bank(2 * (h % 2) + e)
+                wv = s_raw[h][:, e, :].bitcast(F32)
+                for c in range(PASSES):
+                    for u in range(2):
+                        col = (2 * c + u) * P
+                        nc.tensor.transpose(
+                            xt[:, col : col + P], wv[:, 256 * c + u : 256 * (c + 1) : 2], ident[:]
+                        )
+                nc.scalar.copy(
+                    out=s_grp[h][:, e, :, :, :], in_=xt[:].rearrange("p (c u r) -> p c r u", c=PASSES, u=2)
+                )
+
+        def quant_s(h):
+            nc.vector.quantize_mx(
+                out=s_codes[h][:].bitcast(FP8X4),
+                scales=s_scales[h][:],
+                in_=s_grp[h][:].rearrange("p e c r u -> p (e c r u)").bitcast(BF16),
+            )
+
+        def values(g, dq):
+            acc = bank((4 + 4 * g + dq) % 8)
+            cols = slice(dq * P, (dq + 1) * P)
+            for t in range(PACK):
+                h = 2 * g + t // 2
+                for c in range(PASSES):
+                    m = slice(((t % 2) * PASSES + c) * P, ((t % 2) * PASSES + c + 1) * P)
+                    nc.tensor.matmul_mx(
+                        out=acc[:, t * P : (t + 1) * P],
+                        lhsT=s_codes[h][:, m].bitcast(FP8X4),
+                        lhsT_scale=s_scales[h][:, m],
+                        rhs=w_codes[c][:, cols].bitcast(FP8X4),
+                        rhs_scale=w_scales[c][:, cols],
+                        start=(c == 0),
+                        stop=(c == PASSES - 1),
+                    )
+            return acc
+
+        def v_dst(a, g, dq):
+            return v_grp[a][g][dq // 2][:, (dq % 2) * P : (dq % 2 + 1) * P, :]
+
+        def round_v(g, dq, acc, on_vector):
+            src = acc[:].rearrange("p (t d) -> p d t", t=PACK)
+            if on_vector:
+                nc.vector.tensor_copy(out=v_dst(0, g, dq), in_=src)
+            else:
+                nc.scalar.copy(out=v_dst(0, g, dq), in_=src)
+
+        def square_v(g, dq, acc):
+            src = acc[:].rearrange("p (t d) -> p d t", t=PACK)
+            nc.scalar.activation(out=v_dst(1, g, dq), in_=src, func=ACT.Square)
+
+        def quant_v(a, g, x):
+            cols = slice(x * D // 2, (x + 1) * D // 2)
+            nc.vector.quantize_mx(
+                out=v_codes[a][g][:, cols].bitcast(FP8X4),
+                scales=v_scales[a][g][:, cols],
+                in_=v_grp[a][g][x][:].rearrange("p d j -> p (d j)"),
+            )
+
+        outs = (out_0, out_1)
+        res = {}
+        last_of = {}
+        for a in range(2):
+            first = 0
+            for n in STORES[a]:
+                tile_ = sb("res%d_%d" % (a, first), [P, n, D], F32)
+                for e in range(n):
+                    res[a, first + e] = tile_[:, e, :]
+                last_of[a, first + n - 1] = (tile_, first, n)
+                first = first + n
+
+        def attend(a, i, g, acc):
+            nc.tensor.matmul_mx(
+                out=acc[:],
+                lhsT=words[a][:, g, 2 * i * P : 2 * (i + 1) * P].bitcast(FP4X4),
+                lhsT_scale=planes[a][:, g, i * P : (i + 1) * P],
+                rhs=v_codes[a][g][:].bitcast(FP8X4),
+                rhs_scale=v_scales[a][g][:],
+                start=(g == 0),
+                stop=(g == PASSES - 1),
+            )
+
+        def finish(a, i, acc, on_vector):
+            dst = res[a, i]
+            if a == 1:
+                nc.scalar.activation(out=dst, in_=acc[:], func=ACT.Sqrt)
+                nc.vector.tensor_tensor(
+                    out=dst, in0=dst, in1=cont[i // CONTENT_TILES][:, i % CONTENT_TILES, :], op=mybir.AluOpType.mult
+                )
+            elif on_vector:
+                nc.vector.tensor_copy(out=dst, in_=acc[:])
+            else:
+                nc.scalar.copy(out=dst, in_=acc[:])
+            if (a, i) in last_of:
+                tile_, first, n = last_of[a, i]
+                rows = outs[a][first * P : (first + n) * P, :]
+                nc.sync.dma_start(out=rows.rearrange("(a p) d -> p a d", p=P), in_=tile_[:])
+
+        interleave_w(0)
+        turn_s(0)
+        quant_w(0)
+        interleave_w(1)
+        turn_s(1)
+        quant_s(0)
+        quant_w(1)
+        turn_s(2)
+        quant_s(1)
+        quant_s(2)
+        for dq in range(QUARTERS):
+            if dq == 2:
+                turn_s(3)
+                quant_s(3)
+            acc = values(0, dq)
+            square_v(0, dq, acc)
+            round_v(0, dq, acc, True)
+        accs = []
+        for dq in range(QUARTERS):
+            acc = values(1, dq)
+            accs.append(acc)
+            if dq == 0:
+                quant_v(0, 0, 0)
+                quant_v(0, 0, 1)
+            if dq == 3:
+                quant_v(0, 1, 0)
+            round_v(1, dq, acc, dq == 3)
+        early = [bank(4 + i) for i in range(4)]
+        for i in range(4):
+            attend(0, i, 0, early[i])
+        quant_v(0, 1, 1)
+        for dq in range(QUARTERS):
+            square_v(1, dq, accs[dq])
+        for i in range(4):
+            attend(0, i, 1, early[i])
+        for i in range(4):
+            finish(0, i, early[i], True)
+            if i in (0, 2):
+                quant_v(1, i // 2, 0)
+                quant_v(1, i // 2, 1)
+
+        order = [(0, i) for i in range(4, MEAN_LEAD)]
+        for i in range(TILES):
+            order.append((1, i))
+            if MEAN_LEAD + i < TILES - 1:
+                order.append((0, MEAN_LEAD + i))
+        order.append((0, TILES - 1))
+        for step, (a, i) in enumerate(order):
+            acc = bank(step % 8)
+            for g in range(PASSES):
+                attend(a, i, g, acc)
+            finish(a, i, acc, i >= MEAN_LEAD and i % 2 == 1)

@@ -19,11 +19,16 @@ P = 128
 PACK = 4
 K_PASS = P * PACK
 PASSES = 2
+PAIRS = S // (2 * P)
 QUARTERS = D // P
+HALF = D // 2
 TILES = T // P
-STORES = ((1, 1, 2, 2, 2, 2, 2, 2, 1, 1), (2, 2, 2, 2, 2, 2, 2, 1, 1))
 CONTENT_TILES = 4
+BANKS = 8
+RING = BANKS // 2
+MEAN, DEV = 0, 1
 MEAN_LEAD = 6
+VECTOR_EVERY = 3
 
 
 def tile_adaattn_style_moments_s13_kernel(
@@ -35,227 +40,177 @@ def tile_adaattn_style_moments_s13_kernel(
         psum = ctx.enter_context(tc.psum_pool(name="psum", bufs=1))
         ctx.enter_context(tc.manual_schedule())
 
-        def sb(name, shape, dtype):
+        def sbuf(name, shape, dtype):
             return keep.tile(shape, dtype, name=name, align_bytes=64)
 
         def bank(b):
             return psum.tile([P, D], F32, name="bank%d" % b)
 
-        ident = sb("ident", [P, P], F32)
+        ident = sbuf("ident", [P, P], F32)
         make_identity(nc, ident[:])
-        one = sb("one", [P, 8], F32)
-        root = sb("root", [P, 8], F32)
-        nc.gpsimd.memset(one[:], 1.0)
-        nc.scalar.activation(out=root[:], in_=one[:], func=ACT.Sqrt)
 
-        planes = [sb("plane%d" % a, [P, PASSES, T], U8) for a in range(2)]
-        for a in range(2):
-            nc.vector.memset(planes[a][:].rearrange("p g n -> p (g n)").bitcast(I32), 0)
+        map_scales = [sbuf("map_scales%d" % a, [P, PASSES, T], U8) for a in (MEAN, DEV)]
+        for a in (MEAN, DEV):
+            nc.vector.memset(map_scales[a][:].rearrange("p g n -> p (g n)").bitcast(I32), 0)
 
-        w_raw = [sb("w_raw%d" % c, [P, PACK, D], BF16) for c in range(PASSES)]
-        s_raw = [sb("s_raw%d" % h, [P, 2, F], BF16) for h in range(4)]
+        w_raw = [sbuf("w_raw%d" % c, [P, PACK, D], BF16) for c in range(PASSES)]
+        for c in range(PASSES):
+            rows = w_value[c * K_PASS : (c + 1) * K_PASS, :]
+            nc.sync.dma_start(out=w_raw[c][:], in_=rows.rearrange("(p j) d -> p j d", j=PACK))
 
-        def load_w(c):
-            nc.sync.dma_start(
-                out=w_raw[c][:], in_=w_value[c * K_PASS : (c + 1) * K_PASS, :].rearrange("(p j) d -> p j d", j=PACK)
-            )
-
-        def load_s(h):
-            g, half = divmod(h, 2)
+        s_raw = [sbuf("s_raw%d" % n, [P, F], BF16) for n in range(PASSES * PACK)]
+        for g in range(PASSES):
             rows = style[g * K_PASS : (g + 1) * K_PASS, :].rearrange("(m t) k -> m t k", t=PACK)
-            nc.sync.dma_start(out=s_raw[h][:], in_=rows[:, 2 * half : 2 * half + 2, :])
+            for t in range(PACK):
+                nc.sync.dma_start(out=s_raw[PACK * g + t][:], in_=rows[:, t, :])
 
-        load_w(0)
-        load_s(0)
-        load_w(1)
-        load_s(1)
-        load_s(2)
-        load_s(3)
+        map_words = [sbuf("map_words%d" % a, [P, PASSES, 2 * T], U8) for a in (MEAN, DEV)]
+        for a, words_hbm, scales_hbm in ((MEAN, mean_words, mean_scales), (DEV, dev_words, dev_scales)):
+            rows = scales_hbm.rearrange("g q n -> q g n").bitcast(I32)
+            for r in range(4):
+                nc.sync.dma_start(out=map_scales[a][r:P:32, :, :].bitcast(I32), in_=rows[r:16:4, :, :])
+            nc.sync.dma_start(out=map_words[a][:].bitcast(I32), in_=words_hbm.rearrange("g p n -> p g n").bitcast(I32))
 
-        words = [sb("words%d" % a, [P, PASSES, 2 * T], U8) for a in range(2)]
-        for a, (w_hbm, s_hbm) in enumerate(((mean_words, mean_scales), (dev_words, dev_scales))):
-            nc.sync.dma_start(out=words[a][:].bitcast(I32), in_=w_hbm.rearrange("g p n -> p g n").bitcast(I32))
-        for a, (w_hbm, s_hbm) in enumerate(((mean_words, mean_scales), (dev_words, dev_scales))):
-            rows = s_hbm.rearrange("g q n -> q g n").bitcast(I32)
-            for quad in range(4):
-                nc.sync.dma_start(
-                    out=planes[a][32 * quad : 32 * quad + 4, :, :].bitcast(I32), in_=rows[4 * quad : 4 * quad + 4, :, :]
-                )
-        cont = [sb("cont%d" % i, [P, CONTENT_TILES, D], BF16) for i in range(TILES // CONTENT_TILES)]
-        for i in range(TILES // CONTENT_TILES):
-            rows = content[i * CONTENT_TILES * P : (i + 1) * CONTENT_TILES * P, :]
-            nc.sync.dma_start(out=cont[i][:], in_=rows.rearrange("(a p) d -> p a d", p=P))
+        cont = [sbuf("cont%d" % j, [P, CONTENT_TILES, D], BF16) for j in range(TILES // CONTENT_TILES)]
+        for j in range(TILES // CONTENT_TILES):
+            rows = content[j * CONTENT_TILES * P : (j + 1) * CONTENT_TILES * P, :]
+            nc.sync.dma_start(out=cont[j][:], in_=rows.rearrange("(e p) d -> p e d", p=P))
 
-        w_grp = [sb("w_grp%d" % c, [P, D, PACK], BF16) for c in range(PASSES)]
-        w_codes = [sb("w_codes%d" % c, [P, D], U32) for c in range(PASSES)]
-        w_scales = [sb("w_scales%d" % c, [P, D], U8) for c in range(PASSES)]
-        s_grp = [sb("s_grp%d" % h, [P, 2, PASSES, P, 2], F32) for h in range(4)]
-        s_codes = [sb("s_codes%d" % h, [P, 2 * PASSES * P], U32) for h in range(4)]
-        s_scales = [sb("s_scales%d" % h, [P, 2 * PASSES * P], U8) for h in range(4)]
-        v_grp = [[[sb("v_grp%d%d%d" % (a, g, x), [P, D // 2, PACK], BF16) for x in range(2)] for g in range(PASSES)] for a in range(2)]
-        v_codes = [[sb("v_codes%d%d" % (a, g), [P, D], U32) for g in range(PASSES)] for a in range(2)]
-        v_scales = [[sb("v_scales%d%d" % (a, g), [P, D], U8) for g in range(PASSES)] for a in range(2)]
-
-        def interleave_w(c):
+        w_packed = [sbuf("w_packed%d" % c, [P, D, PACK], BF16) for c in range(PASSES)]
+        w_codes = [sbuf("w_codes%d" % c, [P, D], U32) for c in range(PASSES)]
+        w_scales = [sbuf("w_scales%d" % c, [P, D], U8) for c in range(PASSES)]
+        for c in range(PASSES):
             nc.vector.tensor_copy(
-                out=w_grp[c][:].rearrange("p (c i) j -> p c j i", i=4),
-                in_=w_raw[c][:].rearrange("p j (c i) -> p c j i", i=4),
+                out=w_packed[c][:].rearrange("p (b i) j -> p b j i", i=4),
+                in_=w_raw[c][:].rearrange("p j (b i) -> p b j i", i=4),
             )
-
-        def quant_w(c):
+        for c in range(PASSES):
             nc.vector.quantize_mx(
-                out=w_codes[c][:].bitcast(FP8X4), scales=w_scales[c][:], in_=w_grp[c][:].rearrange("p d j -> p (d j)")
+                out=w_codes[c][:].bitcast(FP8X4), scales=w_scales[c][:], in_=w_packed[c][:].rearrange("p d j -> p (d j)")
             )
 
-        def turn_s(h):
+        s_packed = [sbuf("s_packed%d" % h, [P, 2, PASSES, P, 2], F32) for h in range(PAIRS)]
+        s_codes = [sbuf("s_codes%d" % h, [P, 2 * PASSES * P], U32) for h in range(PAIRS)]
+        s_scales = [sbuf("s_scales%d" % h, [P, 2 * PASSES * P], U8) for h in range(PAIRS)]
+        for h in range(PAIRS):
             for e in range(2):
-                xt = bank(2 * (h % 2) + e)
-                wv = s_raw[h][:, e, :].bitcast(F32)
+                turned = bank((2 * h + e) % RING)
+                pairs_of_features = s_raw[2 * h + e][:].bitcast(F32)
                 for c in range(PASSES):
                     for u in range(2):
                         col = (2 * c + u) * P
                         nc.tensor.transpose(
-                            xt[:, col : col + P], wv[:, 256 * c + u : 256 * (c + 1) : 2], ident[:]
+                            turned[:, col : col + P], pairs_of_features[:, 2 * P * c + u : 2 * P * (c + 1) : 2], ident[:]
                         )
                 nc.scalar.copy(
-                    out=s_grp[h][:, e, :, :, :], in_=xt[:].rearrange("p (c u r) -> p c r u", c=PASSES, u=2)
+                    out=s_packed[h][:, e, :, :, :], in_=turned[:].rearrange("p (c u m) -> p c m u", c=PASSES, u=2)
                 )
-
-        def quant_s(h):
             nc.vector.quantize_mx(
                 out=s_codes[h][:].bitcast(FP8X4),
                 scales=s_scales[h][:],
-                in_=s_grp[h][:].rearrange("p e c r u -> p (e c r u)").bitcast(BF16),
+                in_=s_packed[h][:].rearrange("p e c m u -> p (e c m u)").bitcast(BF16),
             )
 
+        v_packed = [
+            [[sbuf("v_packed%d%d%d" % (a, g, x), [P, HALF, PACK], BF16) for x in range(2)] for g in range(PASSES)]
+            for a in (MEAN, DEV)
+        ]
+        v_codes = [[sbuf("v_codes%d%d" % (a, g), [P, D], U32) for g in range(PASSES)] for a in (MEAN, DEV)]
+        v_scales = [[sbuf("v_scales%d%d" % (a, g), [P, D], U8) for g in range(PASSES)] for a in (MEAN, DEV)]
+
         def values(g, dq):
-            acc = bank((4 + 4 * g + dq) % 8)
-            cols = slice(dq * P, (dq + 1) * P)
+            acc = bank((RING * (g + 1) + dq) % BANKS)
+            channels = slice(dq * P, (dq + 1) * P)
             for t in range(PACK):
-                h = 2 * g + t // 2
+                h, e = divmod(PACK * g + t, 2)
                 for c in range(PASSES):
-                    m = slice(((t % 2) * PASSES + c) * P, ((t % 2) * PASSES + c + 1) * P)
+                    tokens = slice((e * PASSES + c) * P, (e * PASSES + c + 1) * P)
                     nc.tensor.matmul_mx(
                         out=acc[:, t * P : (t + 1) * P],
-                        lhsT=s_codes[h][:, m].bitcast(FP8X4),
-                        lhsT_scale=s_scales[h][:, m],
-                        rhs=w_codes[c][:, cols].bitcast(FP8X4),
-                        rhs_scale=w_scales[c][:, cols],
+                        lhsT=s_codes[h][:, tokens].bitcast(FP8X4),
+                        lhsT_scale=s_scales[h][:, tokens],
+                        rhs=w_codes[c][:, channels].bitcast(FP8X4),
+                        rhs_scale=w_scales[c][:, channels],
                         start=(c == 0),
                         stop=(c == PASSES - 1),
                     )
-            return acc
+            return acc[:].rearrange("p (t d) -> p d t", t=PACK)
 
-        def v_dst(a, g, dq):
-            return v_grp[a][g][dq // 2][:, (dq % 2) * P : (dq % 2 + 1) * P, :]
+        def packed_quarter(a, g, dq):
+            return v_packed[a][g][dq // 2][:, (dq % 2) * P : (dq % 2 + 1) * P, :]
 
-        def round_v(g, dq, acc, on_vector):
-            src = acc[:].rearrange("p (t d) -> p d t", t=PACK)
-            if on_vector:
-                nc.vector.tensor_copy(out=v_dst(0, g, dq), in_=src)
-            else:
-                nc.scalar.copy(out=v_dst(0, g, dq), in_=src)
+        def square_v(g, dq, v):
+            nc.scalar.activation(out=packed_quarter(DEV, g, dq), in_=v, func=ACT.Square)
 
-        def square_v(g, dq, acc):
-            src = acc[:].rearrange("p (t d) -> p d t", t=PACK)
-            nc.scalar.activation(out=v_dst(1, g, dq), in_=src, func=ACT.Square)
-
-        def quant_v(a, g, x):
-            cols = slice(x * D // 2, (x + 1) * D // 2)
+        def quantise_v(a, g, x):
+            channels = slice(x * HALF, (x + 1) * HALF)
             nc.vector.quantize_mx(
-                out=v_codes[a][g][:, cols].bitcast(FP8X4),
-                scales=v_scales[a][g][:, cols],
-                in_=v_grp[a][g][x][:].rearrange("p d j -> p (d j)"),
+                out=v_codes[a][g][:, channels].bitcast(FP8X4),
+                scales=v_scales[a][g][:, channels],
+                in_=v_packed[a][g][x][:].rearrange("p d t -> p (d t)"),
             )
-
-        outs = (out_0, out_1)
-        res = {}
-        last_of = {}
-        for a in range(2):
-            first = 0
-            for n in STORES[a]:
-                tile_ = sb("res%d_%d" % (a, first), [P, n, D], F32)
-                for e in range(n):
-                    res[a, first + e] = tile_[:, e, :]
-                last_of[a, first + n - 1] = (tile_, first, n)
-                first = first + n
 
         def attend(a, i, g, acc):
             nc.tensor.matmul_mx(
                 out=acc[:],
-                lhsT=words[a][:, g, 2 * i * P : 2 * (i + 1) * P].bitcast(FP4X4),
-                lhsT_scale=planes[a][:, g, i * P : (i + 1) * P],
+                lhsT=map_words[a][:, g, 2 * i * P : 2 * (i + 1) * P].bitcast(FP4X4),
+                lhsT_scale=map_scales[a][:, g, i * P : (i + 1) * P],
                 rhs=v_codes[a][g][:].bitcast(FP8X4),
                 rhs_scale=v_scales[a][g][:],
                 start=(g == 0),
                 stop=(g == PASSES - 1),
             )
 
-        def finish(a, i, acc, on_vector):
-            dst = res[a, i]
-            if a == 1:
-                nc.scalar.activation(out=dst, in_=acc[:], func=ACT.Sqrt)
+        def finish(a, i, acc):
+            result = sbuf("result%d_%d" % (a, i), [P, D], F32)
+            if a == DEV:
+                nc.scalar.activation(out=result[:], in_=acc[:], func=ACT.Sqrt)
                 nc.vector.tensor_tensor(
-                    out=dst, in0=dst, in1=cont[i // CONTENT_TILES][:, i % CONTENT_TILES, :], op=mybir.AluOpType.mult
+                    out=result[:],
+                    in0=result[:],
+                    in1=cont[i // CONTENT_TILES][:, i % CONTENT_TILES, :],
+                    op=mybir.AluOpType.mult,
                 )
-            elif on_vector:
-                nc.vector.tensor_copy(out=dst, in_=acc[:])
+            elif i < MEAN_LEAD or i % VECTOR_EVERY == VECTOR_EVERY - 1:
+                nc.vector.tensor_copy(out=result[:], in_=acc[:])
             else:
-                nc.scalar.copy(out=dst, in_=acc[:])
-            if (a, i) in last_of:
-                tile_, first, n = last_of[a, i]
-                rows = outs[a][first * P : (first + n) * P, :]
-                nc.sync.dma_start(out=rows.rearrange("(a p) d -> p a d", p=P), in_=tile_[:])
+                nc.scalar.copy(out=result[:], in_=acc[:])
+            nc.sync.dma_start(out=(out_0, out_1)[a][i * P : (i + 1) * P, :], in_=result[:])
 
-        interleave_w(0)
-        turn_s(0)
-        quant_w(0)
-        interleave_w(1)
-        turn_s(1)
-        quant_s(0)
-        quant_w(1)
-        turn_s(2)
-        quant_s(1)
-        quant_s(2)
         for dq in range(QUARTERS):
-            if dq == 2:
-                turn_s(3)
-                quant_s(3)
-            acc = values(0, dq)
-            square_v(0, dq, acc)
-            round_v(0, dq, acc, True)
-        accs = []
-        for dq in range(QUARTERS):
-            acc = values(1, dq)
-            accs.append(acc)
-            if dq == 0:
-                quant_v(0, 0, 0)
-                quant_v(0, 0, 1)
-            if dq == 3:
-                quant_v(0, 1, 0)
-            round_v(1, dq, acc, dq == 3)
-        early = [bank(4 + i) for i in range(4)]
-        for i in range(4):
-            attend(0, i, 0, early[i])
-        quant_v(0, 1, 1)
-        for dq in range(QUARTERS):
-            square_v(1, dq, accs[dq])
-        for i in range(4):
-            attend(0, i, 1, early[i])
-        for i in range(4):
-            finish(0, i, early[i], True)
-            if i in (0, 2):
-                quant_v(1, i // 2, 0)
-                quant_v(1, i // 2, 1)
+            v = values(0, dq)
+            square_v(0, dq, v)
+            nc.vector.tensor_copy(out=packed_quarter(MEAN, 0, dq), in_=v)
 
-        order = [(0, i) for i in range(4, MEAN_LEAD)]
+        quantise_v(MEAN, 0, 0)
+        quantise_v(MEAN, 0, 1)
+        last_group = [values(1, dq) for dq in range(QUARTERS)]
+        for dq in range(QUARTERS - 1):
+            nc.scalar.copy(out=packed_quarter(MEAN, 1, dq), in_=last_group[dq])
+        quantise_v(MEAN, 1, 0)
+        nc.vector.tensor_copy(out=packed_quarter(MEAN, 1, QUARTERS - 1), in_=last_group[QUARTERS - 1])
+        quantise_v(MEAN, 1, 1)
+        for dq in range(QUARTERS):
+            square_v(1, dq, last_group[dq])
+
+        early = [bank(RING + i) for i in range(RING)]
+        for g in range(PASSES):
+            for i in range(RING):
+                attend(MEAN, i, g, early[i])
+        for i in range(RING):
+            finish(MEAN, i, early[i])
+            if i % 2 == 0:
+                quantise_v(DEV, i // 2, 0)
+                quantise_v(DEV, i // 2, 1)
+
+        order = [(MEAN, i) for i in range(RING, MEAN_LEAD)]
+        means_left = TILES - MEAN_LEAD
         for i in range(TILES):
-            order.append((1, i))
-            if MEAN_LEAD + i < TILES - 1:
-                order.append((0, MEAN_LEAD + i))
-        order.append((0, TILES - 1))
+            order.append((DEV, i))
+            if (i + 1) * means_left // TILES > i * means_left // TILES:
+                order.append((MEAN, MEAN_LEAD + i * means_left // TILES))
         for step, (a, i) in enumerate(order):
-            acc = bank(step % 8)
+            acc = bank(step % BANKS)
             for g in range(PASSES):
                 attend(a, i, g, acc)
-            finish(a, i, acc, i >= MEAN_LEAD and i % 2 == 1)
+            finish(a, i, acc)

@@ -23,7 +23,7 @@ PAIRS = S // (2 * P)
 QUARTERS = D // P
 HALF = D // 2
 TILES = T // P
-CONTENT_TILES = 4
+CONTENT_TILES = 8
 BANKS = 8
 RING = BANKS // 2
 MEAN, DEV = 0, 1
@@ -58,11 +58,11 @@ def tile_adaattn_style_moments_s13_kernel(
             rows = w_value[c * K_PASS : (c + 1) * K_PASS, :]
             nc.sync.dma_start(out=w_raw[c][:], in_=rows.rearrange("(p j) d -> p j d", j=PACK))
 
-        s_raw = [sbuf("s_raw%d" % n, [P, F], BF16) for n in range(PASSES * PACK)]
-        for g in range(PASSES):
+        s_raw = [sbuf("s_raw%d" % h, [P, 2, F], BF16) for h in range(PAIRS)]
+        for h in range(PAIRS):
+            g, t = divmod(2 * h, PACK)
             rows = style[g * K_PASS : (g + 1) * K_PASS, :].rearrange("(m t) k -> m t k", t=PACK)
-            for t in range(PACK):
-                nc.sync.dma_start(out=s_raw[PACK * g + t][:], in_=rows[:, t, :])
+            nc.sync.dma_start(out=s_raw[h][:], in_=rows[:, t : t + 2, :])
 
         map_words = [sbuf("map_words%d" % a, [P, PASSES, 2 * T], U8) for a in (MEAN, DEV)]
         for a, words_hbm, scales_hbm in ((MEAN, mean_words, mean_scales), (DEV, dev_words, dev_scales)):
@@ -72,9 +72,10 @@ def tile_adaattn_style_moments_s13_kernel(
             nc.sync.dma_start(out=map_words[a][:].bitcast(I32), in_=words_hbm.rearrange("g p n -> p g n").bitcast(I32))
 
         cont = [sbuf("cont%d" % j, [P, CONTENT_TILES, D], BF16) for j in range(TILES // CONTENT_TILES)]
-        for j in range(TILES // CONTENT_TILES):
+
+        def load_content(j):
             rows = content[j * CONTENT_TILES * P : (j + 1) * CONTENT_TILES * P, :]
-            nc.sync.dma_start(out=cont[j][:], in_=rows.rearrange("(e p) d -> p e d", p=P))
+            nc.scalar.dma_start(out=cont[j][:], in_=rows.rearrange("(e p) d -> p e d", p=P))
 
         w_packed = [sbuf("w_packed%d" % c, [P, D, PACK], BF16) for c in range(PASSES)]
         w_codes = [sbuf("w_codes%d" % c, [P, D], U32) for c in range(PASSES)]
@@ -95,7 +96,7 @@ def tile_adaattn_style_moments_s13_kernel(
         for h in range(PAIRS):
             for e in range(2):
                 turned = bank((2 * h + e) % RING)
-                pairs_of_features = s_raw[2 * h + e][:].bitcast(F32)
+                pairs_of_features = s_raw[h][:, e, :].bitcast(F32)
                 for c in range(PASSES):
                     for u in range(2):
                         col = (2 * c + u) * P
@@ -105,6 +106,8 @@ def tile_adaattn_style_moments_s13_kernel(
                 nc.scalar.copy(
                     out=s_packed[h][:, e, :, :, :], in_=turned[:].rearrange("p (c u m) -> p c m u", c=PASSES, u=2)
                 )
+            if h >= PAIRS - 2:
+                load_content(h - (PAIRS - 2))
             nc.vector.quantize_mx(
                 out=s_codes[h][:].bitcast(FP8X4),
                 scales=s_scales[h][:],

from contextlib import ExitStack

import concourse.mybir as mybir
from concourse.masks import make_identity

S, F, D, T = 1024, 1024, 512, 2048
FLOPS = 2 * S * F * D + 2 * 2 * T * S * D

F32 = mybir.dt.float32
BF16 = mybir.dt.bfloat16
I32 = mybir.dt.int32
U32 = mybir.dt.uint32
U8 = mybir.dt.uint8
FP8X4 = mybir.dt.float8_e4m3fn_x4
FP4X4 = mybir.dt.float4_e2m1fn_x4
ACT = mybir.ActivationFunctionType

P = 128
PACK = 4
K_PASS = P * PACK
PASSES = 2
PAIRS = S // (2 * P)
QUARTERS = D // P
HALF = D // 2
TILES = T // P
CONTENT_TILES = 8
BANKS = 8
RING = BANKS // 2
MEAN, DEV = 0, 1
MEAN_LEAD = 6
VECTOR_EVERY = 3


def tile_adaattn_style_moments_s13_kernel(
    tc, style, w_value, mean_words, mean_scales, dev_words, dev_scales, content, out_0, out_1
):
    nc = tc.nc
    with ExitStack() as ctx:
        keep = ctx.enter_context(tc.tile_pool(name="keep", bufs=1))
        psum = ctx.enter_context(tc.psum_pool(name="psum", bufs=1))
        ctx.enter_context(tc.manual_schedule())

        def sbuf(name, shape, dtype):
            return keep.tile(shape, dtype, name=name, align_bytes=64)

        def bank(b):
            return psum.tile([P, D], F32, name="bank%d" % b)

        ident = sbuf("ident", [P, P], F32)
        make_identity(nc, ident[:])

        map_scales = [sbuf("map_scales%d" % a, [P, PASSES, T], U8) for a in (MEAN, DEV)]
        for a in (MEAN, DEV):
            nc.vector.memset(map_scales[a][:].rearrange("p g n -> p (g n)").bitcast(I32), 0)

        w_raw = [sbuf("w_raw%d" % c, [P, PACK, D], BF16) for c in range(PASSES)]
        for c in range(PASSES):
            rows = w_value[c * K_PASS : (c + 1) * K_PASS, :]
            nc.sync.dma_start(out=w_raw[c][:], in_=rows.rearrange("(p j) d -> p j d", j=PACK))

        s_raw = [sbuf("s_raw%d" % h, [P, 2, F], BF16) for h in range(PAIRS)]
        for h in range(PAIRS):
            g, t = divmod(2 * h, PACK)
            rows = style[g * K_PASS : (g + 1) * K_PASS, :].rearrange("(m t) k -> m t k", t=PACK)
            nc.sync.dma_start(out=s_raw[h][:], in_=rows[:, t : t + 2, :])

        map_words = [sbuf("map_words%d" % a, [P, PASSES, 2 * T], U8) for a in (MEAN, DEV)]
        for a, words_hbm, scales_hbm in ((MEAN, mean_words, mean_scales), (DEV, dev_words, dev_scales)):
            rows = scales_hbm.rearrange("g q n -> q g n").bitcast(I32)
            for r in range(4):
                nc.sync.dma_start(out=map_scales[a][r:P:32, :, :].bitcast(I32), in_=rows[r:16:4, :, :])
            nc.sync.dma_start(out=map_words[a][:].bitcast(I32), in_=words_hbm.rearrange("g p n -> p g n").bitcast(I32))

        cont = [sbuf("cont%d" % j, [P, CONTENT_TILES, D], BF16) for j in range(TILES // CONTENT_TILES)]

        def load_content(j):
            rows = content[j * CONTENT_TILES * P : (j + 1) * CONTENT_TILES * P, :]
            nc.scalar.dma_start(out=cont[j][:], in_=rows.rearrange("(e p) d -> p e d", p=P))

        w_packed = [sbuf("w_packed%d" % c, [P, D, PACK], BF16) for c in range(PASSES)]
        w_codes = [sbuf("w_codes%d" % c, [P, D], U32) for c in range(PASSES)]
        w_scales = [sbuf("w_scales%d" % c, [P, D], U8) for c in range(PASSES)]
        for c in range(PASSES):
            nc.vector.tensor_copy(
                out=w_packed[c][:].rearrange("p (b i) j -> p b j i", i=4),
                in_=w_raw[c][:].rearrange("p j (b i) -> p b j i", i=4),
            )
        for c in range(PASSES):
            nc.vector.quantize_mx(
                out=w_codes[c][:].bitcast(FP8X4), scales=w_scales[c][:], in_=w_packed[c][:].rearrange("p d j -> p (d j)")
            )

        s_packed = [sbuf("s_packed%d" % h, [P, 2, PASSES, P, 2], F32) for h in range(PAIRS)]
        s_codes = [sbuf("s_codes%d" % h, [P, 2 * PASSES * P], U32) for h in range(PAIRS)]
        s_scales = [sbuf("s_scales%d" % h, [P, 2 * PASSES * P], U8) for h in range(PAIRS)]
        for h in range(PAIRS):
            for e in range(2):
                turned = bank((2 * h + e) % RING)
                pairs_of_features = s_raw[h][:, e, :].bitcast(F32)
                for c in range(PASSES):
                    for u in range(2):
                        col = (2 * c + u) * P
                        nc.tensor.transpose(
                            turned[:, col : col + P], pairs_of_features[:, 2 * P * c + u : 2 * P * (c + 1) : 2], ident[:]
                        )
                nc.scalar.copy(
                    out=s_packed[h][:, e, :, :, :], in_=turned[:].rearrange("p (c u m) -> p c m u", c=PASSES, u=2)
                )
            if h >= PAIRS - 2:
                load_content(h - (PAIRS - 2))
            nc.vector.quantize_mx(
                out=s_codes[h][:].bitcast(FP8X4),
                scales=s_scales[h][:],
                in_=s_packed[h][:].rearrange("p e c m u -> p (e c m u)").bitcast(BF16),
            )

        v_packed = [
            [[sbuf("v_packed%d%d%d" % (a, g, x), [P, HALF, PACK], BF16) for x in range(2)] for g in range(PASSES)]
            for a in (MEAN, DEV)
        ]
        v_codes = [[sbuf("v_codes%d%d" % (a, g), [P, D], U32) for g in range(PASSES)] for a in (MEAN, DEV)]
        v_scales = [[sbuf("v_scales%d%d" % (a, g), [P, D], U8) for g in range(PASSES)] for a in (MEAN, DEV)]

        def values(g, dq):
            acc = bank((RING * (g + 1) + dq) % BANKS)
            channels = slice(dq * P, (dq + 1) * P)
            for t in range(PACK):
                h, e = divmod(PACK * g + t, 2)
                for c in range(PASSES):
                    tokens = slice((e * PASSES + c) * P, (e * PASSES + c + 1) * P)
                    nc.tensor.matmul_mx(
                        out=acc[:, t * P : (t + 1) * P],
                        lhsT=s_codes[h][:, tokens].bitcast(FP8X4),
                        lhsT_scale=s_scales[h][:, tokens],
                        rhs=w_codes[c][:, channels].bitcast(FP8X4),
                        rhs_scale=w_scales[c][:, channels],
                        start=(c == 0),
                        stop=(c == PASSES - 1),
                    )
            return acc[:].rearrange("p (t d) -> p d t", t=PACK)

        def packed_quarter(a, g, dq):
            return v_packed[a][g][dq // 2][:, (dq % 2) * P : (dq % 2 + 1) * P, :]

        def square_v(g, dq, v):
            nc.scalar.activation(out=packed_quarter(DEV, g, dq), in_=v, func=ACT.Square)

        def quantise_v(a, g, x):
            channels = slice(x * HALF, (x + 1) * HALF)
            nc.vector.quantize_mx(
                out=v_codes[a][g][:, channels].bitcast(FP8X4),
                scales=v_scales[a][g][:, channels],
                in_=v_packed[a][g][x][:].rearrange("p d t -> p (d t)"),
            )

        def attend(a, i, g, acc):
            nc.tensor.matmul_mx(
                out=acc[:],
                lhsT=map_words[a][:, g, 2 * i * P : 2 * (i + 1) * P].bitcast(FP4X4),
                lhsT_scale=map_scales[a][:, g, i * P : (i + 1) * P],
                rhs=v_codes[a][g][:].bitcast(FP8X4),
                rhs_scale=v_scales[a][g][:],
                start=(g == 0),
                stop=(g == PASSES - 1),
            )

        def finish(a, i, acc):
            result = sbuf("result%d_%d" % (a, i), [P, D], F32)
            if a == DEV:
                nc.scalar.activation(out=result[:], in_=acc[:], func=ACT.Sqrt)
                nc.vector.tensor_tensor(
                    out=result[:],
                    in0=result[:],
                    in1=cont[i // CONTENT_TILES][:, i % CONTENT_TILES, :],
                    op=mybir.AluOpType.mult,
                )
            elif i < MEAN_LEAD or i % VECTOR_EVERY == VECTOR_EVERY - 1:
                nc.vector.tensor_copy(out=result[:], in_=acc[:])
            else:
                nc.scalar.copy(out=result[:], in_=acc[:])
            nc.sync.dma_start(out=(out_0, out_1)[a][i * P : (i + 1) * P, :], in_=result[:])

        for dq in range(QUARTERS):
            v = values(0, dq)
            square_v(0, dq, v)
            nc.vector.tensor_copy(out=packed_quarter(MEAN, 0, dq), in_=v)

        quantise_v(MEAN, 0, 0)
        quantise_v(MEAN, 0, 1)
        last_group = [values(1, dq) for dq in range(QUARTERS)]
        for dq in range(QUARTERS - 1):
            nc.scalar.copy(out=packed_quarter(MEAN, 1, dq), in_=last_group[dq])
        quantise_v(MEAN, 1, 0)
        nc.vector.tensor_copy(out=packed_quarter(MEAN, 1, QUARTERS - 1), in_=last_group[QUARTERS - 1])
        quantise_v(MEAN, 1, 1)
        for dq in range(QUARTERS):
            square_v(1, dq, last_group[dq])

        early = [bank(RING + i) for i in range(RING)]
        for g in range(PASSES):
            for i in range(RING):
                attend(MEAN, i, g, early[i])
        for i in range(RING):
            finish(MEAN, i, early[i])
            if i % 2 == 0:
                quantise_v(DEV, i // 2, 0)
                quantise_v(DEV, i // 2, 1)

        order = [(MEAN, i) for i in range(RING, MEAN_LEAD)]
        means_left = TILES - MEAN_LEAD
        for i in range(TILES):
            order.append((DEV, i))
            if (i + 1) * means_left // TILES > i * means_left // TILES:
                order.append((MEAN, MEAN_LEAD + i * means_left // TILES))
        for step, (a, i) in enumerate(order):
            acc = bank(step % BANKS)
            for g in range(PASSES):
                attend(a, i, g, acc)
            finish(a, i, acc)
